import numpy as np
import ml_dtypes


def mxq(x, axis, fmt="e4m3"):
    dtype, down = {"e4m3": (ml_dtypes.float8_e4m3fn, 7), "e5m2": (ml_dtypes.float8_e5m2, 14)}[fmt]
    v = np.moveaxis(np.asarray(x, np.float32).astype(ml_dtypes.bfloat16).astype(np.float64), axis, -1)
    blocks = v.reshape(v.shape[:-1] + (-1, 32))
    amax = np.abs(blocks).max(-1, keepdims=True)
    byte = np.maximum(np.where(amax > 0, np.frexp(amax)[1] - 1 + 127, 0) - down, 1)
    scale = np.exp2(byte - 127.0)
    codes = (blocks / scale).astype(np.float32).astype(dtype).astype(np.float64)
    return np.moveaxis((codes * scale).reshape(v.shape), -1, axis)


WIDE = False


def mx_kscale(k):
    if not WIDE:
        return np.ones(k)
    levels = np.array([10, -10, 5, -5, 0])
    if k % 512:
        return np.exp2(np.random.permutation(np.resize(levels, k // 32))).repeat(32)
    a = np.empty((k // 512, 16))
    for p in range(k // 512):
        a[p, :8] = np.random.permutation(np.resize(levels, 8))
        for g in range(8):
            far = levels[np.abs(levels - a[p, g]) >= 10]
            a[p, g + 8] = far[np.random.randint(len(far))]
    return np.exp2(a.ravel()).repeat(32)


def f64(x):
    return np.asarray(x).astype(np.float64)


def striped(idx):
    return np.tile(idx.reshape(-1, 16).T, (8, 1)).astype(np.uint16)


def unstriped(offs):
    return offs[:16].T.reshape(-1).astype(np.int64)


def silu(v):
    return v / (1.0 + np.exp(-np.maximum(v, -700.0)))


K, T, D, S, V, H, N = 1024, 2048, 8, 4096, 512, 1024, 128


def setup_inputs():
    n = np.random.standard_normal
    s = mx_kscale(K)[:, None]
    u = mx_kscale(H)
    return {
        "xT": (n((K, T)) * s).astype(np.float32),
        "w1": (n((K, H)) / np.sqrt(K) / s * u).astype(np.float32),
        "w2": (n((H, N)) / np.sqrt(H) / u[:, None]).astype(np.float32),
        "offs": striped(np.concatenate([np.random.permutation(T)[:V] for _ in range(D)])),
    }


def reference(xT, w1, w2, offs):
    idx = unstriped(offs)
    x = np.empty((K, V))
    for l in range(D):
        r = l // 4 * (4 * K // D) + l % 4 + 4 * np.arange(K // D)
        x[r] = f64(xT)[r][:, idx[l * V:(l + 1) * V]]
    xq = mxq(x, 0, "e4m3")
    h = silu(mxq(f64(w1), 0, "e4m3").T @ xq)
    return mxq(f64(w2), 0, "e4m3").T @ mxq(h, 0, "e4m3")

@@ -1,0 +1,148 @@
+from contextlib import ExitStack
+
+import concourse.mybir as mybir
+
+K, T, LEVELS, V, H, N = 1024, 2048, 8, 512, 1024, 128
+FLOPS = 2 * K * H * V + 2 * H * N * V
+
+F32 = mybir.dt.float32
+BF16 = mybir.dt.bfloat16
+U32 = mybir.dt.uint32
+U16 = mybir.dt.uint16
+U8 = mybir.dt.uint8
+FP8X4 = mybir.dt.float8_e4m3fn_x4
+SILU = mybir.ActivationFunctionType.Silu
+
+P = 128
+PACK = 4
+K_PASS = P * PACK
+PASSES = K // K_PASS
+H_PASSES = H // K_PASS
+POINTS = 128
+CHUNKS = V // POINTS
+LIST_COLS = V // 16
+LEVEL_ORDER = (4, 5, 6, 0, 1, 2, 3, 7)
+
+
+def tile_picked_grid_mlp_silu_sub_l_kernel(tc, xT, w1, w2, offs, out):
+    nc = tc.nc
+    with ExitStack() as ctx:
+        keep = ctx.enter_context(tc.tile_pool(name="keep", bufs=1))
+        stage = ctx.enter_context(tc.tile_pool(name="stage", bufs=4))
+        acc_pool = ctx.enter_context(tc.psum_pool(name="acc", bufs=8))
+
+        warm = keep.tile([P, 2], F32, name="warm")
+        nc.vector.memset(warm[:], 0.0)
+        nc.scalar.activation(warm[:, 1:2], warm[:, 0:1], SILU)
+
+        offsets = keep.tile([P, LEVELS * LIST_COLS], U16, name="offsets")
+        nc.sync.dma_start(offsets[:], offs)
+
+        w1_view = [w1[k * K_PASS:(k + 1) * K_PASS, :].rearrange("(p j) w -> p j w", j=PACK) for k in range(PASSES)]
+        w1_raw0 = keep.tile([P, PACK, H], F32, name="w1_raw0")
+        nc.sync.dma_start(out=w1_raw0[:], in_=w1_view[0])
+        w1_raw1 = [keep.tile([P, PACK, K_PASS], F32, name=f"w1_raw1_{c}") for c in range(H_PASSES)]
+        nc.sync.dma_start(out=w1_raw1[0][:], in_=w1_view[1][:, :, 0:K_PASS])
+        tables = {}
+        for level in LEVEL_ORDER:
+            g, t = level // PACK, level % PACK
+            table = keep.tile([P, T], F32, name=f"table{level}")
+            rows = xT[g * K_PASS:(g + 1) * K_PASS, :].rearrange("(f j) w -> f j w", j=PACK)
+            nc.sync.dma_start(out=table[:], in_=rows[:, t, :])
+            tables[level] = table
+        for half in range(2):
+            cols = slice(half * 256, (half + 1) * 256)
+            nc.sync.dma_start(out=w1_raw1[1][:, :, cols], in_=w1_view[1][:, :, K_PASS + half * 256:K_PASS + (half + 1) * 256])
+        w2_raw = keep.tile([P, H_PASSES, PACK, N], F32, name="w2_raw")
+        nc.sync.dma_start(out=w2_raw[:], in_=w2.rearrange("(c p j) n -> p c j n", p=P, j=PACK))
+
+        w1_codes = [[keep.tile([P, K_PASS], U32, name=f"w1c{k}{c}", align_bytes=64) for c in range(H_PASSES)] for k in range(PASSES)]
+        w1_scales = [[keep.tile([P, K_PASS], U8, name=f"w1s{k}{c}", align_bytes=64) for c in range(H_PASSES)] for k in range(PASSES)]
+
+        def cast_w1(engine_copy, raw, grouped, m0, m1):
+            engine_copy(
+                out=grouped.rearrange("p (t m j) -> p m t j", t=PACK, j=PACK)[:, m0:m1, :, :],
+                in_=raw.rearrange("p j (m t) -> p m t j", t=PACK)[:, m0:m1, :, :],
+            )
+
+        def quantize(codes, scales, grouped):
+            nc.vector.quantize_mx(out=codes.bitcast(FP8X4), scales=scales, in_=grouped)
+
+        for k, c, raw in ((0, 0, w1_raw0[:, :, 0:K_PASS]), (0, 1, w1_raw0[:, :, K_PASS:H]), (1, 0, w1_raw1[0][:])):
+            grouped = stage.tile([P, K_PASS * PACK], BF16, name="w1_grouped", align_bytes=64)
+            cast_w1(nc.scalar.copy, raw, grouped[:], 0, P)
+            quantize(w1_codes[k][c][:], w1_scales[k][c][:], grouped[:])
+
+        x_codes = [keep.tile([P, V], U32, name=f"xc{g}", align_bytes=64) for g in range(PASSES)]
+        x_scales = [keep.tile([P, V], U8, name=f"xs{g}", align_bytes=64) for g in range(PASSES)]
+        x_grouped = [keep.tile([P, V, PACK], BF16, name=f"xg{g}", align_bytes=64) for g in range(PASSES)]
+        for level in LEVEL_ORDER:
+            g, t = level // PACK, level % PACK
+            pieces = 2 if level == LEVEL_ORDER[-1] else 1
+            for piece in range(pieces):
+                v0, v1 = piece * V // pieces, (piece + 1) * V // pieces
+                l0 = level * LIST_COLS
+                nc.vector.tensor_copy(
+                    x_grouped[g][:, v0:v1, t],
+                    tables[level][:].indirect(offsets[:, l0 + v0 // 16:l0 + v1 // 16]),
+                )
+            if t == PACK - 1:
+                for piece in range(pieces):
+                    cols = slice(piece * V // pieces, (piece + 1) * V // pieces)
+                    quantize(x_codes[g][:, cols], x_scales[g][:, cols], x_grouped[g][:, cols, :].rearrange("p v t -> p (v t)"))
+
+        h_codes, h_scales = {}, {}
+
+        def first_layer(c):
+            for n in range(CHUNKS):
+                pts = slice(n * POINTS, (n + 1) * POINTS)
+                acc = acc_pool.tile([P, PACK, POINTS], F32, name="acc", tag="acc")
+                for t in range(PACK):
+                    cols = slice(t * P, (t + 1) * P)
+                    for k in range(PASSES):
+                        nc.tensor.matmul_mx(
+                            out=acc[:, t, :],
+                            lhsT=w1_codes[k][c][:, cols].bitcast(FP8X4),
+                            lhsT_scale=w1_scales[k][c][:, cols],
+                            rhs=x_codes[k][:, pts].bitcast(FP8X4),
+                            rhs_scale=x_scales[k][:, pts],
+                            start=(k == 0),
+                            stop=(k == PASSES - 1),
+                        )
+                h = stage.tile([P, POINTS, PACK], BF16, name="h", align_bytes=64)
+                nc.scalar.activation(h[:], acc[:].rearrange("p t n -> p n t"), SILU)
+                codes = keep.tile([P, POINTS], U32, name=f"hc{c}{n}", align_bytes=64)
+                scales = keep.tile([P, POINTS], U8, name=f"hs{c}{n}", align_bytes=64)
+                quantize(codes[:], scales[:], h[:].rearrange("p n t -> p (n t)"))
+                h_codes[c, n], h_scales[c, n] = codes, scales
+
+        grouped = stage.tile([P, K_PASS * PACK], BF16, name="w1_grouped", align_bytes=64)
+        for half in range(2):
+            cast_w1(nc.vector.tensor_copy, w1_raw1[1][:], grouped[:], half * 64, (half + 1) * 64)
+        quantize(w1_codes[1][1][:], w1_scales[1][1][:], grouped[:])
+
+        w2_grouped = keep.tile([P, H_PASSES, N, PACK], BF16, name="w2_grouped", align_bytes=64)
+        w2_codes = keep.tile([P, H_PASSES, N], U32, name="w2_codes", align_bytes=64)
+        w2_scales = keep.tile([P, H_PASSES, N], U8, name="w2_scales", align_bytes=64)
+        nc.vector.tensor_copy(w2_grouped[:], w2_raw[:].rearrange("p c j n -> p c n j"))
+        quantize(w2_codes[:].rearrange("p c n -> p (c n)"), w2_scales[:].rearrange("p c n -> p (c n)"),
+                 w2_grouped[:].rearrange("p c n j -> p (c n j)"))
+
+        first_layer(0)
+        first_layer(1)
+
+        for n in range(CHUNKS):
+            acc2 = acc_pool.tile([P, PACK, POINTS], F32, name="acc2", tag="acc")
+            for c in range(H_PASSES):
+                nc.tensor.matmul_mx(
+                    out=acc2[:, 0, :],
+                    lhsT=w2_codes[:, c, :].bitcast(FP8X4),
+                    lhsT_scale=w2_scales[:, c, :],
+                    rhs=h_codes[c, n][:].bitcast(FP8X4),
+                    rhs_scale=h_scales[c, n][:],
+                    start=(c == 0),
+                    stop=(c == H_PASSES - 1),
+                )
+            result = stage.tile([P, POINTS], F32, name="result")
+            nc.vector.tensor_copy(result[:], acc2[:, 0, :])
+            nc.sync.dma_start(out=out[:, n * POINTS:(n + 1) * POINTS], in_=result[:])

@@ -21,7 +21,6 @@ H_PASSES = H // K_PASS
 POINTS = 128
 CHUNKS = V // POINTS
 LIST_COLS = V // 16
-LEVEL_ORDER = (4, 5, 6, 0, 1, 2, 3, 7)
 
 
 def tile_picked_grid_mlp_silu_sub_l_kernel(tc, xT, w1, w2, offs, out):
@@ -36,24 +35,34 @@ def tile_picked_grid_mlp_silu_sub_l_kernel(tc, xT, w1, w2, offs, out):
         nc.scalar.activation(warm[:, 1:2], warm[:, 0:1], SILU)
 
         offsets = keep.tile([P, LEVELS * LIST_COLS], U16, name="offsets")
-        nc.sync.dma_start(offsets[:], offs)
-
         w1_view = [w1[k * K_PASS:(k + 1) * K_PASS, :].rearrange("(p j) w -> p j w", j=PACK) for k in range(PASSES)]
+        x_view = [xT[g * K_PASS:(g + 1) * K_PASS, :].rearrange("(f j) w -> f j w", j=PACK) for g in range(PASSES)]
         w1_raw0 = keep.tile([P, PACK, H], F32, name="w1_raw0")
-        nc.sync.dma_start(out=w1_raw0[:], in_=w1_view[0])
         w1_raw1 = [keep.tile([P, PACK, K_PASS], F32, name=f"w1_raw1_{c}") for c in range(H_PASSES)]
-        nc.sync.dma_start(out=w1_raw1[0][:], in_=w1_view[1][:, :, 0:K_PASS])
-        tables = {}
-        for level in LEVEL_ORDER:
-            g, t = level // PACK, level % PACK
-            table = keep.tile([P, T], F32, name=f"table{level}")
-            rows = xT[g * K_PASS:(g + 1) * K_PASS, :].rearrange("(f j) w -> f j w", j=PACK)
-            nc.sync.dma_start(out=table[:], in_=rows[:, t, :])
-            tables[level] = table
-        for half in range(2):
-            cols = slice(half * 256, (half + 1) * 256)
-            nc.sync.dma_start(out=w1_raw1[1][:, :, cols], in_=w1_view[1][:, :, K_PASS + half * 256:K_PASS + (half + 1) * 256])
         w2_raw = keep.tile([P, H_PASSES, PACK, N], F32, name="w2_raw")
+        tables = {}
+
+        def load_levels(first, count):
+            g, t = first // PACK, first % PACK
+            tile = keep.tile([P, count, T], F32, name=f"table{first}")
+            nc.sync.dma_start(out=tile[:], in_=x_view[g][:, t:t + count, :])
+            for i in range(count):
+                tables[first + i] = tile[:, i, :]
+
+        def load_w1_late(c, a, b):
+            nc.sync.dma_start(out=w1_raw1[c][:, :, a:b], in_=w1_view[1][:, :, c * K_PASS + a:c * K_PASS + b])
+
+        nc.sync.dma_start(offsets[:], offs)
+        load_levels(4, 2)
+        nc.sync.dma_start(out=w1_raw0[:], in_=w1_view[0])
+        load_w1_late(0, 0, 512)
+        load_levels(0, 2)
+        load_levels(2, 1)
+        load_levels(3, 1)
+        load_levels(6, 1)
+        load_levels(7, 1)
+        load_w1_late(1, 0, 256)
+        load_w1_late(1, 256, 512)
         nc.sync.dma_start(out=w2_raw[:], in_=w2.rearrange("(c p j) n -> p c j n", p=P, j=PACK))
 
         w1_codes = [[keep.tile([P, K_PASS], U32, name=f"w1c{k}{c}", align_bytes=64) for c in range(H_PASSES)] for k in range(PASSES)]
@@ -68,30 +77,56 @@ def tile_picked_grid_mlp_silu_sub_l_kernel(tc, xT, w1, w2, offs, out):
         def quantize(codes, scales, grouped):
             nc.vector.quantize_mx(out=codes.bitcast(FP8X4), scales=scales, in_=grouped)
 
-        for k, c, raw in ((0, 0, w1_raw0[:, :, 0:K_PASS]), (0, 1, w1_raw0[:, :, K_PASS:H]), (1, 0, w1_raw1[0][:])):
-            grouped = stage.tile([P, K_PASS * PACK], BF16, name="w1_grouped", align_bytes=64)
-            cast_w1(nc.scalar.copy, raw, grouped[:], 0, P)
-            quantize(w1_codes[k][c][:], w1_scales[k][c][:], grouped[:])
-
         x_codes = [keep.tile([P, V], U32, name=f"xc{g}", align_bytes=64) for g in range(PASSES)]
         x_scales = [keep.tile([P, V], U8, name=f"xs{g}", align_bytes=64) for g in range(PASSES)]
         x_grouped = [keep.tile([P, V, PACK], BF16, name=f"xg{g}", align_bytes=64) for g in range(PASSES)]
-        for level in LEVEL_ORDER:
+
+        def look_up(level, pieces=1):
             g, t = level // PACK, level % PACK
-            pieces = 2 if level == LEVEL_ORDER[-1] else 1
             for piece in range(pieces):
                 v0, v1 = piece * V // pieces, (piece + 1) * V // pieces
                 l0 = level * LIST_COLS
                 nc.vector.tensor_copy(
                     x_grouped[g][:, v0:v1, t],
-                    tables[level][:].indirect(offsets[:, l0 + v0 // 16:l0 + v1 // 16]),
+                    tables[level].indirect(offsets[:, l0 + v0 // 16:l0 + v1 // 16]),
                 )
-            if t == PACK - 1:
-                for piece in range(pieces):
-                    cols = slice(piece * V // pieces, (piece + 1) * V // pieces)
-                    quantize(x_codes[g][:, cols], x_scales[g][:, cols], x_grouped[g][:, cols, :].rearrange("p v t -> p (v t)"))
 
-        h_codes, h_scales = {}, {}
+        def quantize_x(g, pieces=1):
+            for piece in range(pieces):
+                cols = slice(piece * V // pieces, (piece + 1) * V // pieces)
+                quantize(x_codes[g][:, cols], x_scales[g][:, cols], x_grouped[g][:, cols, :].rearrange("p v t -> p (v t)"))
+
+        def w1_group(k, c, raw, shares):
+            grouped = keep.tile([P, K_PASS * PACK], BF16, name=f"w1g{k}{c}", align_bytes=64)
+            for engine_copy, m0, m1 in shares:
+                cast_w1(engine_copy, raw, grouped[:], m0, m1)
+            quantize(w1_codes[k][c][:], w1_scales[k][c][:], grouped[:])
+
+        w2_grouped = keep.tile([P, H_PASSES, N, PACK], BF16, name="w2_grouped", align_bytes=64)
+        w2_codes = keep.tile([P, H_PASSES, N], U32, name="w2_codes", align_bytes=64)
+        w2_scales = keep.tile([P, H_PASSES, N], U8, name="w2_scales", align_bytes=64)
+
+        def w2_group():
+            nc.vector.tensor_copy(w2_grouped[:], w2_raw[:].rearrange("p c j n -> p c n j"))
+            quantize(w2_codes[:].rearrange("p c n -> p (c n)"), w2_scales[:].rearrange("p c n -> p (c n)"),
+                     w2_grouped[:].rearrange("p c n j -> p (c n j)"))
+
+        def warm_up():
+            idle = acc_pool.tile([P, V], F32, name="idle", tag="acc")
+            for turn in range(4):
+                nc.tensor.matmul_mx(
+                    out=idle[:],
+                    lhsT=w1_codes[0][0][:, 0:P].bitcast(FP8X4),
+                    lhsT_scale=w1_scales[0][0][:, 0:P],
+                    rhs=x_codes[0][:].bitcast(FP8X4),
+                    rhs_scale=x_scales[0][:],
+                    start=True,
+                    stop=True,
+                )
+
+        h = [keep.tile([P, H_PASSES, POINTS, PACK], BF16, name=f"h{n}", align_bytes=64) for n in range(CHUNKS)]
+        h_codes = [keep.tile([P, H_PASSES, POINTS], U32, name=f"hc{n}", align_bytes=64) for n in range(CHUNKS)]
+        h_scales = [keep.tile([P, H_PASSES, POINTS], U8, name=f"hs{n}", align_bytes=64) for n in range(CHUNKS)]
 
         def first_layer(c):
             for n in range(CHUNKS):
@@ -109,37 +144,42 @@ def tile_picked_grid_mlp_silu_sub_l_kernel(tc, xT, w1, w2, offs, out):
                             start=(k == 0),
                             stop=(k == PASSES - 1),
                         )
-                h = stage.tile([P, POINTS, PACK], BF16, name="h", align_bytes=64)
-                nc.scalar.activation(h[:], acc[:].rearrange("p t n -> p n t"), SILU)
-                codes = keep.tile([P, POINTS], U32, name=f"hc{c}{n}", align_bytes=64)
-                scales = keep.tile([P, POINTS], U8, name=f"hs{c}{n}", align_bytes=64)
-                quantize(codes[:], scales[:], h[:].rearrange("p n t -> p (n t)"))
-                h_codes[c, n], h_scales[c, n] = codes, scales
+                nc.scalar.activation(h[n][:, c], acc[:].rearrange("p t n -> p n t"), SILU)
 
-        grouped = stage.tile([P, K_PASS * PACK], BF16, name="w1_grouped", align_bytes=64)
-        for half in range(2):
-            cast_w1(nc.vector.tensor_copy, w1_raw1[1][:], grouped[:], half * 64, (half + 1) * 64)
-        quantize(w1_codes[1][1][:], w1_scales[1][1][:], grouped[:])
-
-        w2_grouped = keep.tile([P, H_PASSES, N, PACK], BF16, name="w2_grouped", align_bytes=64)
-        w2_codes = keep.tile([P, H_PASSES, N], U32, name="w2_codes", align_bytes=64)
-        w2_scales = keep.tile([P, H_PASSES, N], U8, name="w2_scales", align_bytes=64)
-        nc.vector.tensor_copy(w2_grouped[:], w2_raw[:].rearrange("p c j n -> p c n j"))
-        quantize(w2_codes[:].rearrange("p c n -> p (c n)"), w2_scales[:].rearrange("p c n -> p (c n)"),
-                 w2_grouped[:].rearrange("p c n j -> p (c n j)"))
-
+        look_up(4)
+        look_up(5)
+        w1_group(0, 1, w1_raw0[:, :, K_PASS:H], [(nc.vector.tensor_copy, 0, P)])
+        w1_group(0, 0, w1_raw0[:, :, 0:K_PASS], [(nc.scalar.copy, 0, P)])
+        w1_group(1, 0, w1_raw1[0][:], [(nc.scalar.copy, 0, P)])
+        look_up(0)
+        look_up(1)
+        look_up(2)
+        look_up(3)
+        quantize_x(0)
+        warm_up()
+        look_up(6)
+        look_up(7, 2)
+        quantize_x(1, 2)
+        w1_group(1, 1, w1_raw1[1][:], [(nc.vector.tensor_copy, 0, 64), (nc.vector.tensor_copy, 64, P)])
+        w2_group()
         first_layer(0)
         first_layer(1)
 
         for n in range(CHUNKS):
+            if n < 2:
+                quantize(h_codes[n][:].rearrange("p c n -> p (c n)"), h_scales[n][:].rearrange("p c n -> p (c n)"),
+                         h[n][:].rearrange("p c n t -> p (c n t)"))
+            else:
+                for c in range(H_PASSES):
+                    quantize(h_codes[n][:, c], h_scales[n][:, c], h[n][:, c].rearrange("p n t -> p (n t)"))
             acc2 = acc_pool.tile([P, PACK, POINTS], F32, name="acc2", tag="acc")
             for c in range(H_PASSES):
                 nc.tensor.matmul_mx(
                     out=acc2[:, 0, :],
                     lhsT=w2_codes[:, c, :].bitcast(FP8X4),
                     lhsT_scale=w2_scales[:, c, :],
-                    rhs=h_codes[c, n][:].bitcast(FP8X4),
-                    rhs_scale=h_scales[c, n][:],
+                    rhs=h_codes[n][:, c, :].bitcast(FP8X4),
+                    rhs_scale=h_scales[n][:, c, :],
                     start=(c == 0),
                     stop=(c == H_PASSES - 1),
                 )

@@ -53,10 +53,11 @@ def tile_picked_grid_mlp_silu_sub_l_kernel(tc, xT, w1, w2, offs, out):
             nc.sync.dma_start(out=w1_raw1[c][:, :, a:b], in_=w1_view[1][:, :, c * K_PASS + a:c * K_PASS + b])
 
         nc.sync.dma_start(offsets[:], offs)
-        load_levels(4, 2)
         nc.sync.dma_start(out=w1_raw0[:], in_=w1_view[0])
         load_w1_late(0, 0, 512)
-        load_levels(0, 2)
+        load_levels(4, 2)
+        load_levels(0, 1)
+        load_levels(1, 1)
         load_levels(2, 1)
         load_levels(3, 1)
         load_levels(6, 1)
@@ -146,11 +147,11 @@ def tile_picked_grid_mlp_silu_sub_l_kernel(tc, xT, w1, w2, offs, out):
                         )
                 nc.scalar.activation(h[n][:, c], acc[:].rearrange("p t n -> p n t"), SILU)
 
+        w1_group(0, 0, w1_raw0[:, :, 0:K_PASS], [(nc.vector.tensor_copy, 0, P)])
+        w1_group(0, 1, w1_raw0[:, :, K_PASS:H], [(nc.vector.tensor_copy, 0, P)])
+        w1_group(1, 0, w1_raw1[0][:], [(nc.vector.tensor_copy, 0, P)])
         look_up(4)
         look_up(5)
-        w1_group(0, 1, w1_raw0[:, :, K_PASS:H], [(nc.vector.tensor_copy, 0, P)])
-        w1_group(0, 0, w1_raw0[:, :, 0:K_PASS], [(nc.scalar.copy, 0, P)])
-        w1_group(1, 0, w1_raw1[0][:], [(nc.scalar.copy, 0, P)])
         look_up(0)
         look_up(1)
         look_up(2)

@@ -17,106 +17,106 @@ P = 128
 PACK = 4
 K_PASS = P * PACK
 PASSES = K // K_PASS
-H_PASSES = H // K_PASS
+HALVES = H // K_PASS
+HALF_COLS = K_PASS // 2
 POINTS = 128
 CHUNKS = V // POINTS
 LIST_COLS = V // 16
+WARM_UPS = 4
+EARLY_STORED = 2
 
 
 def tile_picked_grid_mlp_silu_sub_l_kernel(tc, xT, w1, w2, offs, out):
     nc = tc.nc
     with ExitStack() as ctx:
         keep = ctx.enter_context(tc.tile_pool(name="keep", bufs=1))
-        stage = ctx.enter_context(tc.tile_pool(name="stage", bufs=4))
-        acc_pool = ctx.enter_context(tc.psum_pool(name="acc", bufs=8))
+        banks = ctx.enter_context(tc.psum_pool(name="banks", bufs=8))
 
-        warm = keep.tile([P, 2], F32, name="warm")
-        nc.vector.memset(warm[:], 0.0)
-        nc.scalar.activation(warm[:, 1:2], warm[:, 0:1], SILU)
+        table_loader = keep.tile([P, 2], F32, name="table_loader")
+        nc.vector.memset(table_loader[:], 0.0)
+        nc.scalar.activation(table_loader[:, 1:2], table_loader[:, 0:1], SILU)
+
+        w1_rows = [w1[k * K_PASS:(k + 1) * K_PASS, :].rearrange("(p j) w -> p j w", j=PACK) for k in range(PASSES)]
+        xT_rows = [xT[g * K_PASS:(g + 1) * K_PASS, :].rearrange("(f j) w -> f j w", j=PACK) for g in range(PASSES)]
 
         offsets = keep.tile([P, LEVELS * LIST_COLS], U16, name="offsets")
-        w1_view = [w1[k * K_PASS:(k + 1) * K_PASS, :].rearrange("(p j) w -> p j w", j=PACK) for k in range(PASSES)]
-        x_view = [xT[g * K_PASS:(g + 1) * K_PASS, :].rearrange("(f j) w -> f j w", j=PACK) for g in range(PASSES)]
-        w1_raw0 = keep.tile([P, PACK, H], F32, name="w1_raw0")
-        w1_raw1 = [keep.tile([P, PACK, K_PASS], F32, name=f"w1_raw1_{c}") for c in range(H_PASSES)]
-        w2_raw = keep.tile([P, H_PASSES, PACK, N], F32, name="w2_raw")
+        nc.sync.dma_start(offsets[:], offs)
+
+        w1_first = keep.tile([P, PACK, H], F32, name="w1_first")
+        nc.sync.dma_start(out=w1_first[:], in_=w1_rows[0])
+        w1_second = [keep.tile([P, PACK, K_PASS], F32, name=f"w1_second{c}") for c in range(HALVES)]
+        nc.sync.dma_start(out=w1_second[0][:], in_=w1_rows[1][:, :, 0:K_PASS])
+
         tables = {}
 
-        def load_levels(first, count):
+        def load_tables(first, count):
             g, t = first // PACK, first % PACK
-            tile = keep.tile([P, count, T], F32, name=f"table{first}")
-            nc.sync.dma_start(out=tile[:], in_=x_view[g][:, t:t + count, :])
+            tile = keep.tile([P, count, T], F32, name=f"tables{first}")
+            nc.sync.dma_start(out=tile[:], in_=xT_rows[g][:, t:t + count, :])
             for i in range(count):
                 tables[first + i] = tile[:, i, :]
 
-        def load_w1_late(c, a, b):
-            nc.sync.dma_start(out=w1_raw1[c][:, :, a:b], in_=w1_view[1][:, :, c * K_PASS + a:c * K_PASS + b])
+        load_tables(4, 2)
+        for level in (0, 1, 2, 3, 6, 7):
+            load_tables(level, 1)
 
-        nc.sync.dma_start(offsets[:], offs)
-        nc.sync.dma_start(out=w1_raw0[:], in_=w1_view[0])
-        load_w1_late(0, 0, 512)
-        load_levels(4, 2)
-        load_levels(0, 1)
-        load_levels(1, 1)
-        load_levels(2, 1)
-        load_levels(3, 1)
-        load_levels(6, 1)
-        load_levels(7, 1)
-        load_w1_late(1, 0, 256)
-        load_w1_late(1, 256, 512)
+        for a in range(0, K_PASS, HALF_COLS):
+            nc.sync.dma_start(out=w1_second[1][:, :, a:a + HALF_COLS],
+                              in_=w1_rows[1][:, :, K_PASS + a:K_PASS + a + HALF_COLS])
+        w2_raw = keep.tile([P, HALVES, PACK, N], F32, name="w2_raw")
         nc.sync.dma_start(out=w2_raw[:], in_=w2.rearrange("(c p j) n -> p c j n", p=P, j=PACK))
-
-        w1_codes = [[keep.tile([P, K_PASS], U32, name=f"w1c{k}{c}", align_bytes=64) for c in range(H_PASSES)] for k in range(PASSES)]
-        w1_scales = [[keep.tile([P, K_PASS], U8, name=f"w1s{k}{c}", align_bytes=64) for c in range(H_PASSES)] for k in range(PASSES)]
-
-        def cast_w1(engine_copy, raw, grouped, m0, m1):
-            engine_copy(
-                out=grouped.rearrange("p (t m j) -> p m t j", t=PACK, j=PACK)[:, m0:m1, :, :],
-                in_=raw.rearrange("p j (m t) -> p m t j", t=PACK)[:, m0:m1, :, :],
-            )
 
         def quantize(codes, scales, grouped):
             nc.vector.quantize_mx(out=codes.bitcast(FP8X4), scales=scales, in_=grouped)
 
-        x_codes = [keep.tile([P, V], U32, name=f"xc{g}", align_bytes=64) for g in range(PASSES)]
-        x_scales = [keep.tile([P, V], U8, name=f"xs{g}", align_bytes=64) for g in range(PASSES)]
-        x_grouped = [keep.tile([P, V, PACK], BF16, name=f"xg{g}", align_bytes=64) for g in range(PASSES)]
+        w1_codes = [[keep.tile([P, K_PASS], U32, name=f"w1_codes{k}{c}", align_bytes=64) for c in range(HALVES)]
+                    for k in range(PASSES)]
+        w1_scales = [[keep.tile([P, K_PASS], U8, name=f"w1_scales{k}{c}", align_bytes=64) for c in range(HALVES)]
+                     for k in range(PASSES)]
 
-        def look_up(level, pieces=1):
-            g, t = level // PACK, level % PACK
-            for piece in range(pieces):
-                v0, v1 = piece * V // pieces, (piece + 1) * V // pieces
-                l0 = level * LIST_COLS
-                nc.vector.tensor_copy(
-                    x_grouped[g][:, v0:v1, t],
-                    tables[level].indirect(offsets[:, l0 + v0 // 16:l0 + v1 // 16]),
+        def prepare_w1(k, c, raw, parts=1, copy=nc.vector.tensor_copy):
+            grouped = keep.tile([P, K_PASS * PACK], BF16, name=f"w1_grouped{k}{c}", align_bytes=64)
+            for part in range(parts):
+                m = slice(part * P // parts, (part + 1) * P // parts)
+                copy(
+                    out=grouped[:].rearrange("p (t m j) -> p m t j", t=PACK, j=PACK)[:, m, :, :],
+                    in_=raw.rearrange("p j (m t) -> p m t j", t=PACK)[:, m, :, :],
                 )
-
-        def quantize_x(g, pieces=1):
-            for piece in range(pieces):
-                cols = slice(piece * V // pieces, (piece + 1) * V // pieces)
-                quantize(x_codes[g][:, cols], x_scales[g][:, cols], x_grouped[g][:, cols, :].rearrange("p v t -> p (v t)"))
-
-        def w1_group(k, c, raw, shares):
-            grouped = keep.tile([P, K_PASS * PACK], BF16, name=f"w1g{k}{c}", align_bytes=64)
-            for engine_copy, m0, m1 in shares:
-                cast_w1(engine_copy, raw, grouped[:], m0, m1)
             quantize(w1_codes[k][c][:], w1_scales[k][c][:], grouped[:])
 
-        w2_grouped = keep.tile([P, H_PASSES, N, PACK], BF16, name="w2_grouped", align_bytes=64)
-        w2_codes = keep.tile([P, H_PASSES, N], U32, name="w2_codes", align_bytes=64)
-        w2_scales = keep.tile([P, H_PASSES, N], U8, name="w2_scales", align_bytes=64)
+        x_grouped = [keep.tile([P, V, PACK], BF16, name=f"x_grouped{g}", align_bytes=64) for g in range(PASSES)]
+        x_codes = [keep.tile([P, V], U32, name=f"x_codes{g}", align_bytes=64) for g in range(PASSES)]
+        x_scales = [keep.tile([P, V], U8, name=f"x_scales{g}", align_bytes=64) for g in range(PASSES)]
 
-        def w2_group():
+        def look_up(level, parts=1):
+            g, t = level // PACK, level % PACK
+            for part in range(parts):
+                v0, v1 = part * V // parts, (part + 1) * V // parts
+                first = level * LIST_COLS
+                nc.vector.tensor_copy(
+                    x_grouped[g][:, v0:v1, t],
+                    tables[level].indirect(offsets[:, first + v0 // 16:first + v1 // 16]),
+                )
+
+        def quantize_x(g, parts=1):
+            for part in range(parts):
+                v = slice(part * V // parts, (part + 1) * V // parts)
+                quantize(x_codes[g][:, v], x_scales[g][:, v], x_grouped[g][:, v, :].rearrange("p v t -> p (v t)"))
+
+        w2_grouped = keep.tile([P, HALVES, N, PACK], BF16, name="w2_grouped", align_bytes=64)
+        w2_codes = keep.tile([P, HALVES, N], U32, name="w2_codes", align_bytes=64)
+        w2_scales = keep.tile([P, HALVES, N], U8, name="w2_scales", align_bytes=64)
+
+        def prepare_w2():
             nc.vector.tensor_copy(w2_grouped[:], w2_raw[:].rearrange("p c j n -> p c n j"))
             quantize(w2_codes[:].rearrange("p c n -> p (c n)"), w2_scales[:].rearrange("p c n -> p (c n)"),
                      w2_grouped[:].rearrange("p c n j -> p (c n j)"))
 
         def warm_up():
-            idle = acc_pool.tile([P, V], F32, name="idle", tag="acc")
-            for turn in range(4):
+            spare = banks.tile([P, V], F32, name="spare", tag="bank")
+            for turn in range(WARM_UPS):
                 nc.tensor.matmul_mx(
-                    out=idle[:],
+                    out=spare[:],
                     lhsT=w1_codes[0][0][:, 0:P].bitcast(FP8X4),
                     lhsT_scale=w1_scales[0][0][:, 0:P],
                     rhs=x_codes[0][:].bitcast(FP8X4),
@@ -125,65 +125,64 @@ def tile_picked_grid_mlp_silu_sub_l_kernel(tc, xT, w1, w2, offs, out):
                     stop=True,
                 )
 
-        h = [keep.tile([P, H_PASSES, POINTS, PACK], BF16, name=f"h{n}", align_bytes=64) for n in range(CHUNKS)]
-        h_codes = [keep.tile([P, H_PASSES, POINTS], U32, name=f"hc{n}", align_bytes=64) for n in range(CHUNKS)]
-        h_scales = [keep.tile([P, H_PASSES, POINTS], U8, name=f"hs{n}", align_bytes=64) for n in range(CHUNKS)]
+        h = [keep.tile([P, HALVES, POINTS, PACK], BF16, name=f"h{n}", align_bytes=64) for n in range(CHUNKS)]
+        h_codes = [keep.tile([P, HALVES, POINTS], U32, name=f"h_codes{n}", align_bytes=64) for n in range(CHUNKS)]
+        h_scales = [keep.tile([P, HALVES, POINTS], U8, name=f"h_scales{n}", align_bytes=64) for n in range(CHUNKS)]
 
         def first_layer(c):
             for n in range(CHUNKS):
-                pts = slice(n * POINTS, (n + 1) * POINTS)
-                acc = acc_pool.tile([P, PACK, POINTS], F32, name="acc", tag="acc")
+                v = slice(n * POINTS, (n + 1) * POINTS)
+                bank = banks.tile([P, PACK, POINTS], F32, name="bank", tag="bank")
                 for t in range(PACK):
-                    cols = slice(t * P, (t + 1) * P)
+                    channels = slice(t * P, (t + 1) * P)
                     for k in range(PASSES):
                         nc.tensor.matmul_mx(
-                            out=acc[:, t, :],
-                            lhsT=w1_codes[k][c][:, cols].bitcast(FP8X4),
-                            lhsT_scale=w1_scales[k][c][:, cols],
-                            rhs=x_codes[k][:, pts].bitcast(FP8X4),
-                            rhs_scale=x_scales[k][:, pts],
+                            out=bank[:, t, :],
+                            lhsT=w1_codes[k][c][:, channels].bitcast(FP8X4),
+                            lhsT_scale=w1_scales[k][c][:, channels],
+                            rhs=x_codes[k][:, v].bitcast(FP8X4),
+                            rhs_scale=x_scales[k][:, v],
                             start=(k == 0),
                             stop=(k == PASSES - 1),
                         )
-                nc.scalar.activation(h[n][:, c], acc[:].rearrange("p t n -> p n t"), SILU)
+                nc.scalar.activation(h[n][:, c], bank[:].rearrange("p t v -> p v t"), SILU)
 
-        w1_group(0, 0, w1_raw0[:, :, 0:K_PASS], [(nc.vector.tensor_copy, 0, P)])
-        w1_group(0, 1, w1_raw0[:, :, K_PASS:H], [(nc.vector.tensor_copy, 0, P)])
-        w1_group(1, 0, w1_raw1[0][:], [(nc.vector.tensor_copy, 0, P)])
-        look_up(4)
-        look_up(5)
-        look_up(0)
-        look_up(1)
-        look_up(2)
-        look_up(3)
+        prepare_w1(0, 0, w1_first[:, :, 0:K_PASS], copy=nc.scalar.copy)
+        prepare_w1(0, 1, w1_first[:, :, K_PASS:H])
+        prepare_w1(1, 0, w1_second[0][:])
+        for level in (4, 5, 0, 1, 2, 3):
+            look_up(level)
         quantize_x(0)
         warm_up()
         look_up(6)
-        look_up(7, 2)
-        quantize_x(1, 2)
-        w1_group(1, 1, w1_raw1[1][:], [(nc.vector.tensor_copy, 0, 64), (nc.vector.tensor_copy, 64, P)])
-        w2_group()
-        first_layer(0)
-        first_layer(1)
+        look_up(7, parts=2)
+        quantize_x(1, parts=2)
+        prepare_w1(1, 1, w1_second[1][:], parts=2)
+        prepare_w2()
+        for c in range(HALVES):
+            first_layer(c)
 
+        result = keep.tile([P, CHUNKS, POINTS], F32, name="result", align_bytes=64)
         for n in range(CHUNKS):
-            if n < 2:
-                quantize(h_codes[n][:].rearrange("p c n -> p (c n)"), h_scales[n][:].rearrange("p c n -> p (c n)"),
-                         h[n][:].rearrange("p c n t -> p (c n t)"))
+            if n < CHUNKS // 2:
+                quantize(h_codes[n][:].rearrange("p c v -> p (c v)"), h_scales[n][:].rearrange("p c v -> p (c v)"),
+                         h[n][:].rearrange("p c v t -> p (c v t)"))
             else:
-                for c in range(H_PASSES):
-                    quantize(h_codes[n][:, c], h_scales[n][:, c], h[n][:, c].rearrange("p n t -> p (n t)"))
-            acc2 = acc_pool.tile([P, PACK, POINTS], F32, name="acc2", tag="acc")
-            for c in range(H_PASSES):
+                for c in range(HALVES):
+                    quantize(h_codes[n][:, c], h_scales[n][:, c], h[n][:, c].rearrange("p v t -> p (v t)"))
+            bank = banks.tile([P, PACK, POINTS], F32, name="out_bank", tag="bank")
+            for c in range(HALVES):
                 nc.tensor.matmul_mx(
-                    out=acc2[:, 0, :],
+                    out=bank[:, 0, :],
                     lhsT=w2_codes[:, c, :].bitcast(FP8X4),
                     lhsT_scale=w2_scales[:, c, :],
                     rhs=h_codes[n][:, c, :].bitcast(FP8X4),
                     rhs_scale=h_scales[n][:, c, :],
                     start=(c == 0),
-                    stop=(c == H_PASSES - 1),
+                    stop=(c == HALVES - 1),
                 )
-            result = stage.tile([P, POINTS], F32, name="result")
-            nc.vector.tensor_copy(result[:], acc2[:, 0, :])
-            nc.sync.dma_start(out=out[:, n * POINTS:(n + 1) * POINTS], in_=result[:])
+            nc.vector.tensor_copy(result[:, n, :], bank[:, 0, :])
+            if n >= EARLY_STORED - 1:
+                first = 0 if n == EARLY_STORED - 1 else n
+                nc.sync.dma_start(out=out[:, first * POINTS:(n + 1) * POINTS],
+                                  in_=result[:, first:n + 1, :].rearrange("p n v -> p (n v)"))

from contextlib import ExitStack

import concourse.mybir as mybir

K, T, LEVELS, V, H, N = 1024, 2048, 8, 512, 1024, 128
FLOPS = 2 * K * H * V + 2 * H * N * V

F32 = mybir.dt.float32
BF16 = mybir.dt.bfloat16
U32 = mybir.dt.uint32
U16 = mybir.dt.uint16
U8 = mybir.dt.uint8
FP8X4 = mybir.dt.float8_e4m3fn_x4
SILU = mybir.ActivationFunctionType.Silu

P = 128
PACK = 4
K_PASS = P * PACK
PASSES = K // K_PASS
HALVES = H // K_PASS
HALF_COLS = K_PASS // 2
POINTS = 128
CHUNKS = V // POINTS
LIST_COLS = V // 16
WARM_UPS = 4
EARLY_STORED = 2


def tile_picked_grid_mlp_silu_sub_l_kernel(tc, xT, w1, w2, offs, out):
    nc = tc.nc
    with ExitStack() as ctx:
        keep = ctx.enter_context(tc.tile_pool(name="keep", bufs=1))
        banks = ctx.enter_context(tc.psum_pool(name="banks", bufs=8))

        table_loader = keep.tile([P, 2], F32, name="table_loader")
        nc.vector.memset(table_loader[:], 0.0)
        nc.scalar.activation(table_loader[:, 1:2], table_loader[:, 0:1], SILU)

        w1_rows = [w1[k * K_PASS:(k + 1) * K_PASS, :].rearrange("(p j) w -> p j w", j=PACK) for k in range(PASSES)]
        xT_rows = [xT[g * K_PASS:(g + 1) * K_PASS, :].rearrange("(f j) w -> f j w", j=PACK) for g in range(PASSES)]

        offsets = keep.tile([P, LEVELS * LIST_COLS], U16, name="offsets")
        nc.sync.dma_start(offsets[:], offs)

        w1_first = keep.tile([P, PACK, H], F32, name="w1_first")
        nc.sync.dma_start(out=w1_first[:], in_=w1_rows[0])
        w1_second = [keep.tile([P, PACK, K_PASS], F32, name=f"w1_second{c}") for c in range(HALVES)]
        nc.sync.dma_start(out=w1_second[0][:], in_=w1_rows[1][:, :, 0:K_PASS])

        tables = {}

        def load_tables(first, count):
            g, t = first // PACK, first % PACK
            tile = keep.tile([P, count, T], F32, name=f"tables{first}")
            nc.sync.dma_start(out=tile[:], in_=xT_rows[g][:, t:t + count, :])
            for i in range(count):
                tables[first + i] = tile[:, i, :]

        load_tables(4, 2)
        for level in (0, 1, 2, 3, 6, 7):
            load_tables(level, 1)

        for a in range(0, K_PASS, HALF_COLS):
            nc.sync.dma_start(out=w1_second[1][:, :, a:a + HALF_COLS],
                              in_=w1_rows[1][:, :, K_PASS + a:K_PASS + a + HALF_COLS])
        w2_raw = keep.tile([P, HALVES, PACK, N], F32, name="w2_raw")
        nc.sync.dma_start(out=w2_raw[:], in_=w2.rearrange("(c p j) n -> p c j n", p=P, j=PACK))

        def quantize(codes, scales, grouped):
            nc.vector.quantize_mx(out=codes.bitcast(FP8X4), scales=scales, in_=grouped)

        w1_codes = [[keep.tile([P, K_PASS], U32, name=f"w1_codes{k}{c}", align_bytes=64) for c in range(HALVES)]
                    for k in range(PASSES)]
        w1_scales = [[keep.tile([P, K_PASS], U8, name=f"w1_scales{k}{c}", align_bytes=64) for c in range(HALVES)]
                     for k in range(PASSES)]

        def prepare_w1(k, c, raw, parts=1, copy=nc.vector.tensor_copy):
            grouped = keep.tile([P, K_PASS * PACK], BF16, name=f"w1_grouped{k}{c}", align_bytes=64)
            for part in range(parts):
                m = slice(part * P // parts, (part + 1) * P // parts)
                copy(
                    out=grouped[:].rearrange("p (t m j) -> p m t j", t=PACK, j=PACK)[:, m, :, :],
                    in_=raw.rearrange("p j (m t) -> p m t j", t=PACK)[:, m, :, :],
                )
            quantize(w1_codes[k][c][:], w1_scales[k][c][:], grouped[:])

        x_grouped = [keep.tile([P, V, PACK], BF16, name=f"x_grouped{g}", align_bytes=64) for g in range(PASSES)]
        x_codes = [keep.tile([P, V], U32, name=f"x_codes{g}", align_bytes=64) for g in range(PASSES)]
        x_scales = [keep.tile([P, V], U8, name=f"x_scales{g}", align_bytes=64) for g in range(PASSES)]

        def look_up(level, parts=1):
            g, t = level // PACK, level % PACK
            for part in range(parts):
                v0, v1 = part * V // parts, (part + 1) * V // parts
                first = level * LIST_COLS
                nc.vector.tensor_copy(
                    x_grouped[g][:, v0:v1, t],
                    tables[level].indirect(offsets[:, first + v0 // 16:first + v1 // 16]),
                )

        def quantize_x(g, parts=1):
            for part in range(parts):
                v = slice(part * V // parts, (part + 1) * V // parts)
                quantize(x_codes[g][:, v], x_scales[g][:, v], x_grouped[g][:, v, :].rearrange("p v t -> p (v t)"))

        w2_grouped = keep.tile([P, HALVES, N, PACK], BF16, name="w2_grouped", align_bytes=64)
        w2_codes = keep.tile([P, HALVES, N], U32, name="w2_codes", align_bytes=64)
        w2_scales = keep.tile([P, HALVES, N], U8, name="w2_scales", align_bytes=64)

        def prepare_w2():
            nc.vector.tensor_copy(w2_grouped[:], w2_raw[:].rearrange("p c j n -> p c n j"))
            quantize(w2_codes[:].rearrange("p c n -> p (c n)"), w2_scales[:].rearrange("p c n -> p (c n)"),
                     w2_grouped[:].rearrange("p c n j -> p (c n j)"))

        def warm_up():
            spare = banks.tile([P, V], F32, name="spare", tag="bank")
            for turn in range(WARM_UPS):
                nc.tensor.matmul_mx(
                    out=spare[:],
                    lhsT=w1_codes[0][0][:, 0:P].bitcast(FP8X4),
                    lhsT_scale=w1_scales[0][0][:, 0:P],
                    rhs=x_codes[0][:].bitcast(FP8X4),
                    rhs_scale=x_scales[0][:],
                    start=True,
                    stop=True,
                )

        h = [keep.tile([P, HALVES, POINTS, PACK], BF16, name=f"h{n}", align_bytes=64) for n in range(CHUNKS)]
        h_codes = [keep.tile([P, HALVES, POINTS], U32, name=f"h_codes{n}", align_bytes=64) for n in range(CHUNKS)]
        h_scales = [keep.tile([P, HALVES, POINTS], U8, name=f"h_scales{n}", align_bytes=64) for n in range(CHUNKS)]

        def first_layer(c):
            for n in range(CHUNKS):
                v = slice(n * POINTS, (n + 1) * POINTS)
                bank = banks.tile([P, PACK, POINTS], F32, name="bank", tag="bank")
                for t in range(PACK):
                    channels = slice(t * P, (t + 1) * P)
                    for k in range(PASSES):
                        nc.tensor.matmul_mx(
                            out=bank[:, t, :],
                            lhsT=w1_codes[k][c][:, channels].bitcast(FP8X4),
                            lhsT_scale=w1_scales[k][c][:, channels],
                            rhs=x_codes[k][:, v].bitcast(FP8X4),
                            rhs_scale=x_scales[k][:, v],
                            start=(k == 0),
                            stop=(k == PASSES - 1),
                        )
                nc.scalar.activation(h[n][:, c], bank[:].rearrange("p t v -> p v t"), SILU)

        prepare_w1(0, 0, w1_first[:, :, 0:K_PASS], copy=nc.scalar.copy)
        prepare_w1(0, 1, w1_first[:, :, K_PASS:H])
        prepare_w1(1, 0, w1_second[0][:])
        for level in (4, 5, 0, 1, 2, 3):
            look_up(level)
        quantize_x(0)
        warm_up()
        look_up(6)
        look_up(7, parts=2)
        quantize_x(1, parts=2)
        prepare_w1(1, 1, w1_second[1][:], parts=2)
        prepare_w2()
        for c in range(HALVES):
            first_layer(c)

        result = keep.tile([P, CHUNKS, POINTS], F32, name="result", align_bytes=64)
        for n in range(CHUNKS):
            if n < CHUNKS // 2:
                quantize(h_codes[n][:].rearrange("p c v -> p (c v)"), h_scales[n][:].rearrange("p c v -> p (c v)"),
                         h[n][:].rearrange("p c v t -> p (c v t)"))
            else:
                for c in range(HALVES):
                    quantize(h_codes[n][:, c], h_scales[n][:, c], h[n][:, c].rearrange("p v t -> p (v t)"))
            bank = banks.tile([P, PACK, POINTS], F32, name="out_bank", tag="bank")
            for c in range(HALVES):
                nc.tensor.matmul_mx(
                    out=bank[:, 0, :],
                    lhsT=w2_codes[:, c, :].bitcast(FP8X4),
                    lhsT_scale=w2_scales[:, c, :],
                    rhs=h_codes[n][:, c, :].bitcast(FP8X4),
                    rhs_scale=h_scales[n][:, c, :],
                    start=(c == 0),
                    stop=(c == HALVES - 1),
                )
            nc.vector.tensor_copy(result[:, n, :], bank[:, 0, :])
            if n >= EARLY_STORED - 1:
                first = 0 if n == EARLY_STORED - 1 else n
                nc.sync.dma_start(out=out[:, first * POINTS:(n + 1) * POINTS],
                                  in_=result[:, first:n + 1, :].rearrange("p n v -> p (n v)"))
